import numpy as np
import ml_dtypes


def mxq(x, axis, fmt="e4m3"):
    dtype, down = {"e4m3": (ml_dtypes.float8_e4m3fn, 7), "e5m2": (ml_dtypes.float8_e5m2, 14)}[fmt]
    v = np.moveaxis(np.asarray(x, np.float32).astype(ml_dtypes.bfloat16).astype(np.float64), axis, -1)
    blocks = v.reshape(v.shape[:-1] + (-1, 32))
    amax = np.abs(blocks).max(-1, keepdims=True)
    byte = np.maximum(np.where(amax > 0, np.frexp(amax)[1] - 1 + 127, 0) - down, 1)
    scale = np.exp2(byte - 127.0)
    codes = (blocks / scale).astype(np.float32).astype(dtype).astype(np.float64)
    return np.moveaxis((codes * scale).reshape(v.shape), -1, axis)


WIDE = False


def mx_kscale(k):
    if not WIDE:
        return np.ones(k)
    levels = np.array([30, -30])
    if k % 512:
        return np.exp2(np.random.permutation(np.resize(levels, k // 32))).repeat(32)
    a = np.empty((k // 512, 16))
    for p in range(k // 512):
        a[p, :8] = np.random.permutation(np.resize(levels, 8))
        for g in range(8):
            far = levels[np.abs(levels - a[p, g]) >= 10]
            a[p, g + 8] = far[np.random.randint(len(far))]
    return np.exp2(a.ravel()).repeat(32)


def f64(x):
    return np.asarray(x).astype(np.float64)


def striped(idx):
    return np.tile(idx.reshape(-1, 16).T, (8, 1)).astype(np.uint16)


def unstriped(offs):
    return offs[:16].T.reshape(-1).astype(np.int64)


def bf(x):
    return np.asarray(x, np.float32).astype(ml_dtypes.bfloat16)


E2M1 = np.array([0.0, 0.5, 1.0, 1.5, 2.0, 3.0, 4.0, 6.0, -0.0, -0.5, -1.0, -1.5, -2.0, -3.0, -4.0, -6.0])


def pack_weight(w, fmt):
    k, n = w.shape
    w = f64(bf(w)).reshape(k // 32, 32, n)
    amax = np.abs(w).max(1)
    if fmt in ("e4m3", "e5m2"):
        byte = np.frexp(amax)[1] - 1 + 127 - (7 if fmt == "e4m3" else 14)
    else:
        mant, ex = np.frexp(amax / 6.0)
        byte = np.where(mant > 0.5, ex, ex - 1) + 127
    byte = np.clip(np.where(amax > 0, byte, 1), 1, 254)
    scaled = (w * np.exp2(127.0 - byte)[:, None, :]).reshape(k, n).astype(np.float32)
    by_word = np.ascontiguousarray(scaled.reshape(k // 512, 128, 4, n).transpose(0, 1, 3, 2))
    if fmt in ("e4m3", "e5m2"):
        words = by_word.astype(ml_dtypes.float8_e4m3fn if fmt == "e4m3" else ml_dtypes.float8_e5m2).view(np.uint8)
    else:
        c = by_word.astype(ml_dtypes.float4_e2m1fn).view(np.uint8) & 0xF
        words = c[..., 0::2] | (c[..., 1::2] << 4)
    return np.ascontiguousarray(words), np.ascontiguousarray(byte.astype(np.uint8).reshape(k // 512, 16, n))


def unpack_weight(words, scales, fmt):
    g, p, n, _ = words.shape
    if fmt in ("e4m3", "e5m2"):
        vals = np.ascontiguousarray(words).view(ml_dtypes.float8_e4m3fn if fmt == "e4m3" else ml_dtypes.float8_e5m2).astype(np.float64)
    else:
        nib = np.empty((g, p, n, 4), np.uint8)
        nib[..., 0::2] = words & 0xF
        nib[..., 1::2] = words >> 4
        vals = E2M1[nib]
    vals = vals * np.repeat(np.exp2(scales.astype(np.float64) - 127.0), 8, axis=1)[..., None]
    return vals.transpose(0, 1, 3, 2).reshape(g * 512, n)


K, H, N, T, S, T2 = 1024, 1024, 512, 2048, 1024, 2048

def setup_inputs():
    n = np.random.standard_normal
    s = mx_kscale(K)[:, None]
    u = mx_kscale(H)[:, None]
    tab = n((K, T)) * np.exp(1.0 * n((1, T))) * s
    tab_words, tab_scales = pack_weight(tab, "e5m2")
    w1 = n((K, H)) / np.sqrt(K) / s * u.T
    w2 = 4.0 * n((H, N)) / np.sqrt(H) / u
    w3 = 3.0 * n((H, N)) / np.sqrt(H) / u
    w2_words, w2_scales = pack_weight(w2, "e4m3")
    sT = 1.0 / (1.0 + np.exp(-n((H, T))))
    return {
        "tab_words": tab_words, "tab_scales": tab_scales,
        "offs": striped(np.random.permutation(T)[:S]),
        "sT": sT.astype(np.float32),
        "w1": w1.astype(np.float32),
        "w2_words": w2_words, "w2_scales": w2_scales,
        "w3": w3.astype(np.float32),
        "wgo": np.exp(0.3 * n((128, S))).astype(np.float32),
        "offs2": striped(np.random.permutation(T2)[:S]),
    }

def reference(tab_words, tab_scales, offs, sT, w1, w2_words, w2_scales, w3, wgo, offs2):
    v = unpack_weight(tab_words, tab_scales, "e5m2")[:, unstriped(offs)]
    s_ = f64(sT)[:, unstriped(offs)]
    h = mxq(f64(w1), 0, "e4m3").T @ v
    d = mxq(h * (s_ * (1.0 - s_)), 0, "e4m3")
    ym = unpack_weight(w2_words, w2_scales, "e4m3").T @ d
    yr = mxq(f64(w3), 0, "e4m3").T @ d
    y = ym * np.tanh(yr)
    out = np.zeros((N, T2))
    out[:, unstriped(offs2)] = np.tile(f64(wgo), (N // 128, 1)) * y
    return out

@@ -1,0 +1,257 @@
+from contextlib import ExitStack
+
+import concourse.mybir as mybir
+
+K, H, N, T, S, T2 = 1024, 1024, 512, 2048, 1024, 2048
+FLOPS = 2 * K * H * S + 2 * 2 * H * N * S
+
+F32 = mybir.dt.float32
+BF16 = mybir.dt.bfloat16
+I32 = mybir.dt.int32
+U32 = mybir.dt.uint32
+U16 = mybir.dt.uint16
+U8 = mybir.dt.uint8
+E4M3 = mybir.dt.float8_e4m3fn_x4
+E5M2 = mybir.dt.float8_e5m2_x4
+ALU = mybir.AluOpType
+ACT = mybir.ActivationFunctionType
+
+P = 128
+PACK = 4
+PASS = P * PACK
+HALF = 512
+GATE_RING = 4
+RAW_RING = 3
+H_BANKS = 4
+PART_RING = 3
+PAGES = 3
+B_ON_GPSIMD = ()
+
+
+def tile_list_disruption_pair_sensitivity_kernel(
+    tc, tab_words, tab_scales, offs, sT, w1, w2_words, w2_scales, w3, wgo, offs2, out
+):
+    nc = tc.nc
+    with ExitStack() as ctx:
+        sb = ctx.enter_context(tc.tile_pool(name="sb", bufs=1))
+        ps = ctx.enter_context(tc.psum_pool(name="ps", bufs=1))
+
+        def tiles(name, count, shape, dtype):
+            return [sb.tile(shape, dtype, name="%s%d" % (name, i), align_bytes=64) for i in range(count)]
+
+        idx = sb.tile([P, S // 16], U16, name="idx")
+        idx2 = sb.tile([P, S // 16], U16, name="idx2")
+        tab_w = tiles("tab_w", 2, [P, T], U32)
+        tab_s = sb.tile([P, 2, T], U8, name="tab_s", align_bytes=64)
+        v_w = tiles("v_w", 2, [P, S], U32)
+        v_s = tiles("v_s", 2, [P, S], U8)
+        raw = tiles("raw", RAW_RING, [P, PACK, PASS], F32)
+        w_bf = tiles("w_bf", 2, [P, PASS * PACK], BF16)
+        w1_w = tiles("w1_w", 4, [P, PASS], U32)
+        w1_s = tiles("w1_s", 4, [P, PASS], U8)
+        w3_w = tiles("w3_w", 2, [P, N], U32)
+        w3_s = tiles("w3_s", 2, [P, N], U8)
+        w2_w = sb.tile([P, 2, N], U32, name="w2_w", align_bytes=64)
+        w2_s = sb.tile([P, 2, N], U8, name="w2_s", align_bytes=64)
+        wgo_sb = sb.tile([P, S], F32, name="wgo_sb", align_bytes=64)
+        gates = tiles("gates", GATE_RING, [P, T], F32)
+        s_sel = tiles("s_sel", 2 * PACK, [P, S], F32)
+        part = tiles("part", PART_RING, [P, HALF], F32)
+        d_rows = tiles("d_rows", 4, [P, PACK, HALF], BF16)
+        d_bf = tiles("d_bf", 2, [P, HALF * PACK], BF16)
+        d_w = tiles("d_w", 4, [P, HALF], U32)
+        d_s = tiles("d_s", 4, [P, HALF], U8)
+        lim = tiles("lim", 2, [P, HALF], F32)
+        y_sb = tiles("y_sb", 2, [P, HALF], F32)
+        pages = tiles("page", PAGES, [P, T2], F32)
+        h_ps = [ps.tile([P, HALF], F32, name="h_ps%d" % i) for i in range(H_BANKS)]
+        ym_ps = [ps.tile([P, HALF], F32, name="ym_ps%d" % i) for i in range(2)]
+        yr_ps = [ps.tile([P, HALF], F32, name="yr_ps%d" % i) for i in range(2)]
+
+        def load_scale_rows(queue, plane, rows):
+            nc.vector.memset(plane[:].rearrange("p a c -> p (a c)").bitcast(I32), 0)
+            for q in range(4):
+                queue.dma_start(
+                    out=plane[32 * q : 32 * q + 4, :, :].bitcast(I32),
+                    in_=rows[:, 4 * q : 4 * q + 4, :].rearrange("a r c -> r a c").bitcast(I32),
+                )
+
+        def load_weight(i):
+            if i < 4:
+                b, a = divmod(i, 2)
+                rows = w1[a * PASS : (a + 1) * PASS, b * PASS : (b + 1) * PASS]
+            else:
+                rows = w3[(i - 4) * PASS : (i - 3) * PASS, :]
+            nc.sync.dma_start(out=raw[i % RAW_RING][:], in_=rows.rearrange("(p j) c -> p j c", j=PACK))
+
+        def quantize_weight(i):
+            src, grouped = raw[i % RAW_RING], w_bf[i % 2]
+            if i < 4:
+                nc.scalar.copy(
+                    out=grouped[:].rearrange("p (t m j) -> p m j t", t=PACK, j=PACK),
+                    in_=src[:].rearrange("p j (m t) -> p m j t", t=PACK),
+                )
+                words, scales = w1_w[i], w1_s[i]
+            else:
+                nc.scalar.copy(
+                    out=grouped[:].rearrange("p (c i j) -> p c j i", i=PACK, j=PACK),
+                    in_=src[:].rearrange("p j (c i) -> p c j i", i=PACK),
+                )
+                words, scales = w3_w[i - 4], w3_s[i - 4]
+            nc.vector.quantize_mx(out=words[:].bitcast(E4M3), scales=scales[:], in_=grouped[:])
+
+        def load_table(a):
+            nc.sync.dma_start(
+                out=tab_w[a][:].bitcast(I32), in_=tab_words[a].rearrange("p c i -> p (c i)").bitcast(I32)
+            )
+
+        def load_gates(g):
+            b, t = divmod(g, PACK)
+            rows = sT[b * PASS : (b + 1) * PASS, :].rearrange("(p t) c -> p t c", t=PACK)
+            nc.sync.dma_start(out=gates[g % GATE_RING][:], in_=rows[:, t, :])
+
+        def gather_gates(g):
+            nc.vector.tensor_copy(out=s_sel[g][:], in_=gates[g % GATE_RING][:].indirect(idx[:]))
+
+        steps = []
+
+        def gate_step(g, half):
+            b, t = divmod(g, PACK)
+            u = len(steps)
+            steps.append(u)
+            cols = slice(half * HALF, (half + 1) * HALF)
+            bank = h_ps[u % H_BANKS]
+            for a in range(2):
+                nc.tensor.matmul_mx(
+                    out=bank[:],
+                    lhsT=w1_w[2 * b + a][:, t * P : (t + 1) * P].bitcast(E4M3),
+                    lhsT_scale=w1_s[2 * b + a][:, t * P : (t + 1) * P],
+                    rhs=v_w[a][:, cols].bitcast(E5M2),
+                    rhs_scale=v_s[a][:, cols],
+                    start=(a == 0),
+                    stop=(a == 1),
+                )
+            nc.vector.scalar_tensor_tensor(
+                out=part[u % PART_RING][:], in0=s_sel[g][:, cols], scalar=1.0, in1=bank[:],
+                op0=ALU.subtract, op1=ALU.mult,
+            )
+            return (u, g, half)
+
+        def gate_finish(step):
+            u, g, half = step
+            b, t = divmod(g, PACK)
+            cols = slice(half * HALF, (half + 1) * HALF)
+            eng = nc.gpsimd if u in B_ON_GPSIMD else nc.vector
+            eng.tensor_tensor(
+                out=d_rows[2 * b + half][:, t, :], in0=part[u % PART_RING][:], in1=s_sel[g][:, cols], op=ALU.mult
+            )
+
+        def interleave_d(b, half):
+            nc.scalar.activation(
+                out=d_bf[half][:].rearrange("p (c t) -> p c t", t=PACK),
+                in_=d_rows[2 * b + half][:].rearrange("p t c -> p c t"),
+                func=ACT.Copy,
+                scale=-1.0,
+            )
+
+        def quantize_d(b, half):
+            nc.vector.quantize_mx(
+                out=d_w[2 * b + half][:].bitcast(E4M3), scales=d_s[2 * b + half][:], in_=d_bf[half][:]
+            )
+
+        def pair_products(u, nt, half):
+            rows = slice(nt * P, (nt + 1) * P)
+            for bank, words, scales in (
+                (yr_ps[u % 2], [w3_w[0][:], w3_w[1][:]], [w3_s[0][:], w3_s[1][:]]),
+                (ym_ps[u % 2], [w2_w[:, 0, :], w2_w[:, 1, :]], [w2_s[:, 0, :], w2_s[:, 1, :]]),
+            ):
+                for b in range(2):
+                    nc.tensor.matmul_mx(
+                        out=bank[:],
+                        lhsT=words[b][:, rows].bitcast(E4M3),
+                        lhsT_scale=scales[b][:, rows],
+                        rhs=d_w[2 * b + half][:].bitcast(E4M3),
+                        rhs_scale=d_s[2 * b + half][:],
+                        start=(b == 0),
+                        stop=(b == 1),
+                    )
+            nc.scalar.activation(out=lim[u % 2][:], in_=yr_ps[u % 2][:], func=ACT.Tanh)
+            nc.vector.tensor_tensor(out=y_sb[u % 2][:], in0=ym_ps[u % 2][:], in1=lim[u % 2][:], op=ALU.mult)
+
+        def place(u, nt, half):
+            cols = slice(half * HALF, (half + 1) * HALF)
+            page = pages[nt % PAGES]
+            nc.vector.tensor_tensor(
+                out=page[:].indirect(idx2[:, half * HALF // 16 : (half + 1) * HALF // 16]),
+                in0=y_sb[u % 2][:], in1=wgo_sb[:, cols], op=ALU.mult,
+            )
+            if half == 1:
+                nc.sync.dma_start(out=out[nt * P : (nt + 1) * P, :], in_=page[:])
+
+        nc.sync.dma_start(idx[:], offs)
+        load_scale_rows(nc.scalar, tab_s, tab_scales)
+        load_weight(0)
+        load_table(0)
+        load_weight(1)
+        load_table(1)
+        load_gates(0)
+        for page in pages:
+            nc.vector.memset(page[:], 0.0)
+        for a in range(2):
+            nc.vector.tensor_copy(out=v_s[a][:], in_=tab_s[:, a, :].indirect(idx[:]))
+        for a in range(2):
+            nc.vector.tensor_copy(out=v_w[a][:], in_=tab_w[a][:].indirect(idx[:]))
+            quantize_weight(a)
+        load_gates(1)
+        load_gates(2)
+        load_weight(2)
+        load_gates(3)
+        load_weight(3)
+
+        for g in range(PACK):
+            gather_gates(g)
+            load_gates(g + PACK)
+            pair = [gate_step(g, half) for half in range(2)]
+            if g >= 2:
+                quantize_weight(g)
+            for step in pair:
+                gate_finish(step)
+        load_weight(4)
+        load_weight(5)
+        load_scale_rows(nc.sync, w2_s, w2_scales)
+        nc.sync.dma_start(out=w2_w[:].bitcast(I32), in_=w2_words.rearrange("a p c i -> p a (c i)").bitcast(I32))
+        nc.sync.dma_start(out=wgo_sb[:], in_=wgo)
+        nc.sync.dma_start(idx2[:], offs2)
+        for half in range(2):
+            interleave_d(0, half)
+
+        waiting = None
+        for g in range(PACK, 2 * PACK):
+            gather_gates(g)
+            if waiting is not None:
+                gate_finish(waiting)
+            waiting = gate_step(g, 0)
+            if g < PACK + 2:
+                quantize_d(0, g - PACK)
+            else:
+                quantize_weight(g - 2)
+        for g in range(PACK, 2 * PACK):
+            step = gate_step(g, 1)
+            gate_finish(waiting)
+            if g == PACK:
+                interleave_d(1, 0)
+            waiting = step
+            if g == PACK + 2:
+                quantize_d(1, 0)
+        gate_finish(waiting)
+        interleave_d(1, 1)
+
+        order = [(nt, 0) for nt in range(PAGES)] + [(nt, 1) for nt in range(PAGES)]
+        order = order + [(nt, half) for nt in range(PAGES, N // P) for half in range(2)]
+        pair_products(0, *order[0])
+        for u in range(len(order)):
+            if u == 1:
+                quantize_d(1, 1)
+            if u + 1 < len(order):
+                pair_products(u + 1, *order[u + 1])
+            place(u, *order[u])

@@ -20,12 +20,13 @@ P = 128
 PACK = 4
 PASS = P * PACK
 HALF = 512
-GATE_RING = 4
-RAW_RING = 3
+GATE_RING = 8
+RAW_RING = 4
 H_BANKS = 4
-PART_RING = 3
+PART_RING = 4
+SEL_RING = 4
 PAGES = 3
-B_ON_GPSIMD = ()
+GP_STEPS = 11
 
 
 def tile_list_disruption_pair_sensitivity_kernel(
@@ -42,8 +43,9 @@ def tile_list_disruption_pair_sensitivity_kernel(
         idx = sb.tile([P, S // 16], U16, name="idx")
         idx2 = sb.tile([P, S // 16], U16, name="idx2")
         tab_w = tiles("tab_w", 2, [P, T], U32)
-        tab_s = sb.tile([P, 2, T], U8, name="tab_s", align_bytes=64)
+        tab_s = sb.tile([P, T], U8, name="tab_s", align_bytes=64)
         v_w = tiles("v_w", 2, [P, S], U32)
+        sel_s = sb.tile([P, S], U8, name="sel_s", align_bytes=64)
         v_s = tiles("v_s", 2, [P, S], U8)
         raw = tiles("raw", RAW_RING, [P, PACK, PASS], F32)
         w_bf = tiles("w_bf", 2, [P, PASS * PACK], BF16)
@@ -55,9 +57,9 @@ def tile_list_disruption_pair_sensitivity_kernel(
         w2_s = sb.tile([P, 2, N], U8, name="w2_s", align_bytes=64)
         wgo_sb = sb.tile([P, S], F32, name="wgo_sb", align_bytes=64)
         gates = tiles("gates", GATE_RING, [P, T], F32)
-        s_sel = tiles("s_sel", 2 * PACK, [P, S], F32)
+        s_sel = tiles("s_sel", SEL_RING, [P, HALF], F32)
         part = tiles("part", PART_RING, [P, HALF], F32)
-        d_rows = tiles("d_rows", 4, [P, PACK, HALF], BF16)
+        d_rows = tiles("d_rows", 3, [P, PACK, HALF], BF16)
         d_bf = tiles("d_bf", 2, [P, HALF * PACK], BF16)
         d_w = tiles("d_w", 4, [P, HALF], U32)
         d_s = tiles("d_s", 4, [P, HALF], U8)
@@ -110,15 +112,21 @@ def tile_list_disruption_pair_sensitivity_kernel(
             rows = sT[b * PASS : (b + 1) * PASS, :].rearrange("(p t) c -> p t c", t=PACK)
             nc.sync.dma_start(out=gates[g % GATE_RING][:], in_=rows[:, t, :])
 
-        def gather_gates(g):
-            nc.vector.tensor_copy(out=s_sel[g][:], in_=gates[g % GATE_RING][:].indirect(idx[:]))
+        steps = [(g, half) for g in range(PACK) for half in range(2)]
+        steps = steps + [(g, half) for half in range(2) for g in range(PACK, 2 * PACK)]
+        late = len(steps) - PACK
 
-        steps = []
+        def sel_slot(u):
+            return s_sel[u % SEL_RING] if u < late else sel_slot(u - 2)
 
-        def gate_step(g, half):
+        def gather_gates(u):
+            g, half = steps[u]
+            offsets = idx[:, half * HALF // 16 : (half + 1) * HALF // 16]
+            nc.vector.tensor_copy(out=sel_slot(u)[:], in_=gates[g % GATE_RING][:].indirect(offsets))
+
+        def gate_step(u):
+            g, half = steps[u]
             b, t = divmod(g, PACK)
-            u = len(steps)
-            steps.append(u)
             cols = slice(half * HALF, (half + 1) * HALF)
             bank = h_ps[u % H_BANKS]
             for a in range(2):
@@ -132,24 +140,17 @@ def tile_list_disruption_pair_sensitivity_kernel(
                     stop=(a == 1),
                 )
             nc.vector.scalar_tensor_tensor(
-                out=part[u % PART_RING][:], in0=s_sel[g][:, cols], scalar=1.0, in1=bank[:],
+                out=part[u % PART_RING][:], in0=sel_slot(u)[:], scalar=1.0, in1=bank[:],
                 op0=ALU.subtract, op1=ALU.mult,
             )
-            return (u, g, half)
-
-        def gate_finish(step):
-            u, g, half = step
-            b, t = divmod(g, PACK)
-            cols = slice(half * HALF, (half + 1) * HALF)
-            eng = nc.gpsimd if u in B_ON_GPSIMD else nc.vector
-            eng.tensor_tensor(
-                out=d_rows[2 * b + half][:, t, :], in0=part[u % PART_RING][:], in1=s_sel[g][:, cols], op=ALU.mult
+            (nc.gpsimd if u < GP_STEPS else nc.vector).tensor_tensor(
+                out=d_rows[(2 * b + half) % 3][:, t, :], in0=part[u % PART_RING][:], in1=sel_slot(u)[:], op=ALU.mult
             )
 
         def interleave_d(b, half):
             nc.scalar.activation(
                 out=d_bf[half][:].rearrange("p (c t) -> p c t", t=PACK),
-                in_=d_rows[2 * b + half][:].rearrange("p t c -> p c t"),
+                in_=d_rows[(2 * b + half) % 3][:].rearrange("p t c -> p c t"),
                 func=ACT.Copy,
                 scale=-1.0,
             )
@@ -189,61 +190,63 @@ def tile_list_disruption_pair_sensitivity_kernel(
                 nc.sync.dma_start(out=out[nt * P : (nt + 1) * P, :], in_=page[:])
 
         nc.sync.dma_start(idx[:], offs)
-        load_scale_rows(nc.scalar, tab_s, tab_scales)
+        for q in range(4):
+            nc.scalar.dma_start(
+                out=tab_s[32 * q + 24 : 32 * q + 32, :].bitcast(I32),
+                in_=tab_scales[:, 4 * q : 4 * q + 4, :].bitcast(I32),
+            )
+            nc.vector.memset(tab_s[32 * q : 32 * q + 24, :].bitcast(I32), 0)
         load_weight(0)
         load_table(0)
         load_weight(1)
         load_table(1)
         load_gates(0)
+        load_gates(1)
         for page in pages:
-            nc.vector.memset(page[:], 0.0)
+            nc.gpsimd.memset(page[:], 0.0)
+        nc.vector.tensor_copy(out=sel_s[:], in_=tab_s[:].indirect(idx[:]))
         for a in range(2):
-            nc.vector.tensor_copy(out=v_s[a][:], in_=tab_s[:, a, :].indirect(idx[:]))
+            first = 24 + 4 * a
+            nc.vector.memset(v_s[a][:].bitcast(I32), 0)
+            nc.scalar.dma_start(out=v_s[a][0 : P - first, :].bitcast(I32), in_=sel_s[first:P, :].bitcast(I32))
         for a in range(2):
             nc.vector.tensor_copy(out=v_w[a][:], in_=tab_w[a][:].indirect(idx[:]))
             quantize_weight(a)
-        load_gates(1)
-        load_gates(2)
         load_weight(2)
-        load_gates(3)
         load_weight(3)
+        for g in (2, 3, 4):
+            load_gates(g)
 
-        for g in range(PACK):
-            gather_gates(g)
-            load_gates(g + PACK)
-            pair = [gate_step(g, half) for half in range(2)]
-            if g >= 2:
-                quantize_weight(g)
-            for step in pair:
-                gate_finish(step)
-        load_weight(4)
-        load_weight(5)
-        load_scale_rows(nc.sync, w2_s, w2_scales)
-        nc.sync.dma_start(out=w2_w[:].bitcast(I32), in_=w2_words.rearrange("a p c i -> p a (c i)").bitcast(I32))
-        nc.sync.dma_start(out=wgo_sb[:], in_=wgo)
-        nc.sync.dma_start(idx2[:], offs2)
-        for half in range(2):
-            interleave_d(0, half)
-
-        waiting = None
-        for g in range(PACK, 2 * PACK):
-            gather_gates(g)
-            if waiting is not None:
-                gate_finish(waiting)
-            waiting = gate_step(g, 0)
-            if g < PACK + 2:
-                quantize_d(0, g - PACK)
-            else:
-                quantize_weight(g - 2)
-        for g in range(PACK, 2 * PACK):
-            step = gate_step(g, 1)
-            gate_finish(waiting)
-            if g == PACK:
+        gather_gates(0)
+        for u in range(len(steps)):
+            g, half = steps[u]
+            if u + 1 < len(steps):
+                gather_gates(u + 1)
+            gate_step(u)
+            if u in (3, 4):
+                quantize_weight(u - 1)
+            if u == 4:
+                load_weight(4)
+                load_gates(5)
+                load_weight(5)
+                load_gates(6)
+                load_gates(7)
+                load_scale_rows(nc.sync, w2_s, w2_scales)
+                nc.sync.dma_start(
+                    out=w2_w[:].bitcast(I32), in_=w2_words.rearrange("a p c i -> p a (c i)").bitcast(I32)
+                )
+                nc.sync.dma_start(out=wgo_sb[:], in_=wgo)
+                nc.sync.dma_start(idx2[:], offs2)
+            if u in (6, 7):
+                interleave_d(0, u - 6)
+            if u in (8, 9):
+                quantize_d(0, u - 8)
+            if u in (9, 10):
+                quantize_weight(u - 5)
+            if u == 11:
                 interleave_d(1, 0)
-            waiting = step
-            if g == PACK + 2:
+            if u == 13:
                 quantize_d(1, 0)
-        gate_finish(waiting)
         interleave_d(1, 1)
 
         order = [(nt, 0) for nt in range(PAGES)] + [(nt, 1) for nt in range(PAGES)]

@@ -23,10 +23,9 @@ HALF = 512
 GATE_RING = 8
 RAW_RING = 4
 H_BANKS = 4
-PART_RING = 4
+PART_RING = 3
 SEL_RING = 4
-PAGES = 3
-GP_STEPS = 11
+LATE = 13
 
 
 def tile_list_disruption_pair_sensitivity_kernel(
@@ -38,7 +37,8 @@ def tile_list_disruption_pair_sensitivity_kernel(
         ps = ctx.enter_context(tc.psum_pool(name="ps", bufs=1))
 
         def tiles(name, count, shape, dtype):
-            return [sb.tile(shape, dtype, name="%s%d" % (name, i), align_bytes=64) for i in range(count)]
+            names = ["%s%d" % (name, i) for i in range(count)]
+            return [sb.tile(shape, dtype, name=each, tag=each, align_bytes=64) for each in names]
 
         idx = sb.tile([P, S // 16], U16, name="idx")
         idx2 = sb.tile([P, S // 16], U16, name="idx2")
@@ -51,7 +51,7 @@ def tile_list_disruption_pair_sensitivity_kernel(
         w_bf = tiles("w_bf", 2, [P, PASS * PACK], BF16)
         w1_w = tiles("w1_w", 4, [P, PASS], U32)
         w1_s = tiles("w1_s", 4, [P, PASS], U8)
-        w3_w = tiles("w3_w", 2, [P, N], U32)
+        w3_w = []
         w3_s = tiles("w3_s", 2, [P, N], U8)
         w2_w = sb.tile([P, 2, N], U32, name="w2_w", align_bytes=64)
         w2_s = sb.tile([P, 2, N], U8, name="w2_s", align_bytes=64)
@@ -61,11 +61,11 @@ def tile_list_disruption_pair_sensitivity_kernel(
         part = tiles("part", PART_RING, [P, HALF], F32)
         d_rows = tiles("d_rows", 3, [P, PACK, HALF], BF16)
         d_bf = tiles("d_bf", 2, [P, HALF * PACK], BF16)
-        d_w = tiles("d_w", 4, [P, HALF], U32)
+        d_w = {}
         d_s = tiles("d_s", 4, [P, HALF], U8)
         lim = tiles("lim", 2, [P, HALF], F32)
         y_sb = tiles("y_sb", 2, [P, HALF], F32)
-        pages = tiles("page", PAGES, [P, T2], F32)
+        pages = tiles("page", 3, [P, T2], F32)
         h_ps = [ps.tile([P, HALF], F32, name="h_ps%d" % i) for i in range(H_BANKS)]
         ym_ps = [ps.tile([P, HALF], F32, name="ym_ps%d" % i) for i in range(2)]
         yr_ps = [ps.tile([P, HALF], F32, name="yr_ps%d" % i) for i in range(2)]
@@ -86,21 +86,22 @@ def tile_list_disruption_pair_sensitivity_kernel(
                 rows = w3[(i - 4) * PASS : (i - 3) * PASS, :]
             nc.sync.dma_start(out=raw[i % RAW_RING][:], in_=rows.rearrange("(p j) c -> p j c", j=PACK))
 
-        def quantize_weight(i):
+        def cast_weight(i):
             src, grouped = raw[i % RAW_RING], w_bf[i % 2]
             if i < 4:
                 nc.scalar.copy(
                     out=grouped[:].rearrange("p (t m j) -> p m j t", t=PACK, j=PACK),
                     in_=src[:].rearrange("p j (m t) -> p m j t", t=PACK),
                 )
-                words, scales = w1_w[i], w1_s[i]
             else:
                 nc.scalar.copy(
                     out=grouped[:].rearrange("p (c i j) -> p c j i", i=PACK, j=PACK),
                     in_=src[:].rearrange("p j (c i) -> p c j i", i=PACK),
                 )
-                words, scales = w3_w[i - 4], w3_s[i - 4]
-            nc.vector.quantize_mx(out=words[:].bitcast(E4M3), scales=scales[:], in_=grouped[:])
+
+        def quantize_weight(i):
+            words, scales = (w1_w[i][:], w1_s[i]) if i < 4 else (w3_w[i - 4], w3_s[i - 4])
+            nc.vector.quantize_mx(out=words.bitcast(E4M3), scales=scales[:], in_=w_bf[i % 2][:])
 
         def load_table(a):
             nc.sync.dma_start(
@@ -112,12 +113,10 @@ def tile_list_disruption_pair_sensitivity_kernel(
             rows = sT[b * PASS : (b + 1) * PASS, :].rearrange("(p t) c -> p t c", t=PACK)
             nc.sync.dma_start(out=gates[g % GATE_RING][:], in_=rows[:, t, :])
 
-        steps = [(g, half) for g in range(PACK) for half in range(2)]
-        steps = steps + [(g, half) for half in range(2) for g in range(PACK, 2 * PACK)]
-        late = len(steps) - PACK
+        steps = [(g, half) for g in range(6) for half in range(2)] + [(6, 0), (7, 0), (6, 1), (7, 1)]
 
         def sel_slot(u):
-            return s_sel[u % SEL_RING] if u < late else sel_slot(u - 2)
+            return s_sel[min(u, LATE) % SEL_RING]
 
         def gather_gates(u):
             g, half = steps[u]
@@ -143,13 +142,13 @@ def tile_list_disruption_pair_sensitivity_kernel(
                 out=part[u % PART_RING][:], in0=sel_slot(u)[:], scalar=1.0, in1=bank[:],
                 op0=ALU.subtract, op1=ALU.mult,
             )
-            (nc.gpsimd if u < GP_STEPS else nc.vector).tensor_tensor(
+            (nc.gpsimd if u < LATE else nc.vector).tensor_tensor(
                 out=d_rows[(2 * b + half) % 3][:, t, :], in0=part[u % PART_RING][:], in1=sel_slot(u)[:], op=ALU.mult
             )
 
         def interleave_d(b, half):
             nc.scalar.activation(
-                out=d_bf[half][:].rearrange("p (c t) -> p c t", t=PACK),
+                out=d_bf[(2 * b + half) % 3][:].rearrange("p (c t) -> p c t", t=PACK),
                 in_=d_rows[(2 * b + half) % 3][:].rearrange("p t c -> p c t"),
                 func=ACT.Copy,
                 scale=-1.0,
@@ -157,31 +156,25 @@ def tile_list_disruption_pair_sensitivity_kernel(
 
         def quantize_d(b, half):
             nc.vector.quantize_mx(
-                out=d_w[2 * b + half][:].bitcast(E4M3), scales=d_s[2 * b + half][:], in_=d_bf[half][:]
+                out=d_w[b, half].bitcast(E4M3), scales=d_s[2 * b + half][:], in_=d_bf[(2 * b + half) % 3][:]
             )
 
-        def pair_products(u, nt, half):
+        def product(bank, words, scales, nt, half):
             rows = slice(nt * P, (nt + 1) * P)
-            for bank, words, scales in (
-                (yr_ps[u % 2], [w3_w[0][:], w3_w[1][:]], [w3_s[0][:], w3_s[1][:]]),
-                (ym_ps[u % 2], [w2_w[:, 0, :], w2_w[:, 1, :]], [w2_s[:, 0, :], w2_s[:, 1, :]]),
-            ):
-                for b in range(2):
-                    nc.tensor.matmul_mx(
-                        out=bank[:],
-                        lhsT=words[b][:, rows].bitcast(E4M3),
-                        lhsT_scale=scales[b][:, rows],
-                        rhs=d_w[2 * b + half][:].bitcast(E4M3),
-                        rhs_scale=d_s[2 * b + half][:],
-                        start=(b == 0),
-                        stop=(b == 1),
-                    )
-            nc.scalar.activation(out=lim[u % 2][:], in_=yr_ps[u % 2][:], func=ACT.Tanh)
-            nc.vector.tensor_tensor(out=y_sb[u % 2][:], in0=ym_ps[u % 2][:], in1=lim[u % 2][:], op=ALU.mult)
+            for b in range(2):
+                nc.tensor.matmul_mx(
+                    out=bank[:],
+                    lhsT=words[b][:, rows].bitcast(E4M3),
+                    lhsT_scale=scales[b][:, rows],
+                    rhs=d_w[b, half].bitcast(E4M3),
+                    rhs_scale=d_s[2 * b + half][:],
+                    start=(b == 0),
+                    stop=(b == 1),
+                )
 
         def place(u, nt, half):
             cols = slice(half * HALF, (half + 1) * HALF)
-            page = pages[nt % PAGES]
+            page = pages[nt]
             nc.vector.tensor_tensor(
                 out=page[:].indirect(idx2[:, half * HALF // 16 : (half + 1) * HALF // 16]),
                 in0=y_sb[u % 2][:], in1=wgo_sb[:, cols], op=ALU.mult,
@@ -202,59 +195,74 @@ def tile_list_disruption_pair_sensitivity_kernel(
         load_table(1)
         load_gates(0)
         load_gates(1)
-        for page in pages:
-            nc.gpsimd.memset(page[:], 0.0)
         nc.vector.tensor_copy(out=sel_s[:], in_=tab_s[:].indirect(idx[:]))
         for a in range(2):
             first = 24 + 4 * a
             nc.vector.memset(v_s[a][:].bitcast(I32), 0)
             nc.scalar.dma_start(out=v_s[a][0 : P - first, :].bitcast(I32), in_=sel_s[first:P, :].bitcast(I32))
+        for page in pages:
+            nc.vector.memset(page[:], 0.0)
         for a in range(2):
             nc.vector.tensor_copy(out=v_w[a][:], in_=tab_w[a][:].indirect(idx[:]))
+            cast_weight(a)
             quantize_weight(a)
+        pages.append(sb.tile([P, T2], F32, name="page3", tag="tab_w0", align_bytes=64))
+        nc.gpsimd.memset(pages[3][:], 0.0)
+        d_bf.append(sb.tile([P, HALF * PACK], BF16, name="d_bf2", tag="tab_w1", align_bytes=64))
         load_weight(2)
         load_weight(3)
-        for g in (2, 3, 4):
+        for g in (2, 3, 4, 5):
             load_gates(g)
+        load_weight(4)
+        load_gates(6)
+        load_weight(5)
+        load_gates(7)
+        load_scale_rows(nc.sync, w2_s, w2_scales)
+        nc.sync.dma_start(out=w2_w[:].bitcast(I32), in_=w2_words.rearrange("a p c i -> p a (c i)").bitcast(I32))
+        nc.sync.dma_start(out=wgo_sb[:], in_=wgo)
+        nc.sync.dma_start(idx2[:], offs2)
 
         gather_gates(0)
-        for u in range(len(steps)):
-            g, half = steps[u]
-            if u + 1 < len(steps):
+        for u in range(LATE + 1):
+            if u < LATE:
                 gather_gates(u + 1)
             gate_step(u)
             if u in (3, 4):
+                cast_weight(u - 1)
                 quantize_weight(u - 1)
-            if u == 4:
-                load_weight(4)
-                load_gates(5)
-                load_weight(5)
-                load_gates(6)
-                load_gates(7)
-                load_scale_rows(nc.sync, w2_s, w2_scales)
-                nc.sync.dma_start(
-                    out=w2_w[:].bitcast(I32), in_=w2_words.rearrange("a p c i -> p a (c i)").bitcast(I32)
-                )
-                nc.sync.dma_start(out=wgo_sb[:], in_=wgo)
-                nc.sync.dma_start(idx2[:], offs2)
             if u in (6, 7):
                 interleave_d(0, u - 6)
-            if u in (8, 9):
-                quantize_d(0, u - 8)
-            if u in (9, 10):
-                quantize_weight(u - 5)
-            if u == 11:
-                interleave_d(1, 0)
-            if u == 13:
-                quantize_d(1, 0)
+            if u in (10, 11):
+                cast_weight(u - 6)
+        interleave_d(1, 0)
+
+        gather_gates(LATE + 1)
+        late_w = sb.tile([P, 3, HALF], U32, name="late_w", tag="gates6", align_bytes=64)
+        w3_w.extend([late_w[:, 0, :], late_w[:, 1, :]])
+        d_rest = tiles("d_w", 2, [P, HALF], U32)
+        d_w[0, 0], d_w[1, 0], d_w[1, 1] = late_w[:, 2, :], d_rest[0][:], d_rest[1][:]
+        quantize_d(0, 0)
+        quantize_weight(4)
+        quantize_weight(5)
+        quantize_d(1, 0)
+        gate_step(LATE + 1)
+        gather_gates(LATE + 2)
+        last_w = sb.tile([P, HALF], U32, name="last_w", tag="gates7", align_bytes=64)
+        d_w[0, 1] = last_w[:]
+        quantize_d(0, 1)
+        gate_step(LATE + 2)
         interleave_d(1, 1)
 
-        order = [(nt, 0) for nt in range(PAGES)] + [(nt, 1) for nt in range(PAGES)]
-        order = order + [(nt, half) for nt in range(PAGES, N // P) for half in range(2)]
-        pair_products(0, *order[0])
-        for u in range(len(order)):
-            if u == 1:
-                quantize_d(1, 1)
-            if u + 1 < len(order):
-                pair_products(u + 1, *order[u + 1])
-            place(u, *order[u])
+        w2_parts = [w2_w[:, 0, :], w2_w[:, 1, :]], [w2_s[:, 0, :], w2_s[:, 1, :]]
+        for half in range(2):
+            for first in range(0, N // P, 2):
+                for u in range(2):
+                    product(yr_ps[u], w3_w, w3_s, first + u, half)
+                    nc.scalar.activation(out=lim[u][:], in_=yr_ps[u][:], func=ACT.Tanh)
+                for u in range(2):
+                    product(ym_ps[u], *w2_parts, first + u, half)
+                    nc.vector.tensor_tensor(out=y_sb[u][:], in0=ym_ps[u][:], in1=lim[u][:], op=ALU.mult)
+                if half == 0 and first == 0:
+                    quantize_d(1, 1)
+                for u in range(2):
+                    place(u, first + u, half)

@@ -64,7 +64,7 @@ def tile_list_disruption_pair_sensitivity_kernel(
         d_w = {}
         d_s = tiles("d_s", 4, [P, HALF], U8)
         lim = tiles("lim", 2, [P, HALF], F32)
-        y_sb = tiles("y_sb", 2, [P, HALF], F32)
+        y_sb = tiles("y_sb", 3, [P, HALF], F32)
         pages = tiles("page", 3, [P, T2], F32)
         h_ps = [ps.tile([P, HALF], F32, name="h_ps%d" % i) for i in range(H_BANKS)]
         ym_ps = [ps.tile([P, HALF], F32, name="ym_ps%d" % i) for i in range(2)]
@@ -172,16 +172,6 @@ def tile_list_disruption_pair_sensitivity_kernel(
                     stop=(b == 1),
                 )
 
-        def place(u, nt, half):
-            cols = slice(half * HALF, (half + 1) * HALF)
-            page = pages[nt]
-            nc.vector.tensor_tensor(
-                out=page[:].indirect(idx2[:, half * HALF // 16 : (half + 1) * HALF // 16]),
-                in0=y_sb[u % 2][:], in1=wgo_sb[:, cols], op=ALU.mult,
-            )
-            if half == 1:
-                nc.sync.dma_start(out=out[nt * P : (nt + 1) * P, :], in_=page[:])
-
         nc.sync.dma_start(idx[:], offs)
         for q in range(4):
             nc.scalar.dma_start(
@@ -254,15 +244,28 @@ def tile_list_disruption_pair_sensitivity_kernel(
         interleave_d(1, 1)
 
         w2_parts = [w2_w[:, 0, :], w2_w[:, 1, :]], [w2_s[:, 0, :], w2_s[:, 1, :]]
-        for half in range(2):
-            for first in range(0, N // P, 2):
-                for u in range(2):
-                    product(yr_ps[u], w3_w, w3_s, first + u, half)
-                    nc.scalar.activation(out=lim[u][:], in_=yr_ps[u][:], func=ACT.Tanh)
-                for u in range(2):
-                    product(ym_ps[u], *w2_parts, first + u, half)
-                    nc.vector.tensor_tensor(out=y_sb[u][:], in0=ym_ps[u][:], in1=lim[u][:], op=ALU.mult)
-                if half == 0 and first == 0:
-                    quantize_d(1, 1)
-                for u in range(2):
-                    place(u, first + u, half)
+        ym_sb = sb.tile([P, 2, HALF], F32, name="ym_sb", tag="raw2", align_bytes=64)
+        factor = sb.tile([P, 2, HALF], F32, name="factor", tag="raw3", align_bytes=64)
+        units = [(nt, half) for half in range(2) for nt in range(N // P)]
+        for u, (nt, half) in enumerate(units):
+            cols = slice(half * HALF, (half + 1) * HALF)
+            product(yr_ps[u % 2], w3_w, w3_s, nt, half)
+            nc.scalar.activation(out=lim[u % 2][:], in_=yr_ps[u % 2][:], func=ACT.Tanh)
+            product(ym_ps[u % 2], *w2_parts, nt, half)
+            (nc.vector if u == 0 else nc.gpsimd).tensor_tensor(
+                out=factor[:, u % 2, :], in0=lim[u % 2][:], in1=wgo_sb[:, cols], op=ALU.mult
+            )
+            if u == 2:
+                quantize_d(1, 1)
+                y_held = sb.tile([P, 2, HALF], F32, name="y_held", tag="d_bf0", align_bytes=64)
+            y = y_held[:, u - 2, :] if u in (2, 3) else y_sb[u % 3][:]
+            if u in (0, 2):
+                nc.vector.tensor_tensor(out=y, in0=ym_ps[0][:], in1=factor[:, 0, :], op=ALU.mult)
+            else:
+                nc.scalar.copy(out=ym_sb[:, u % 2, :], in_=ym_ps[u % 2][:])
+                nc.gpsimd.tensor_tensor(out=y, in0=ym_sb[:, u % 2, :], in1=factor[:, u % 2, :], op=ALU.mult)
+            nc.vector.tensor_copy(
+                out=pages[nt][:].indirect(idx2[:, half * HALF // 16 : (half + 1) * HALF // 16]), in_=y
+            )
+            if half == 1:
+                nc.sync.dma_start(out=out[nt * P : (nt + 1) * P, :], in_=pages[nt][:])

from contextlib import ExitStack

import concourse.mybir as mybir

K, H, N, T, S, T2 = 1024, 1024, 512, 2048, 1024, 2048
FLOPS = 2 * K * H * S + 2 * 2 * H * N * S

F32 = mybir.dt.float32
BF16 = mybir.dt.bfloat16
I32 = mybir.dt.int32
U32 = mybir.dt.uint32
U16 = mybir.dt.uint16
U8 = mybir.dt.uint8
E4M3 = mybir.dt.float8_e4m3fn_x4
E5M2 = mybir.dt.float8_e5m2_x4
ALU = mybir.AluOpType
ACT = mybir.ActivationFunctionType

P = 128
PACK = 4
PASS = P * PACK
HALF = 512
GATE_RING = 8
RAW_RING = 4
H_BANKS = 4
PART_RING = 3
SEL_RING = 4
LATE = 13


def tile_list_disruption_pair_sensitivity_kernel(
    tc, tab_words, tab_scales, offs, sT, w1, w2_words, w2_scales, w3, wgo, offs2, out
):
    nc = tc.nc
    with ExitStack() as ctx:
        sb = ctx.enter_context(tc.tile_pool(name="sb", bufs=1))
        ps = ctx.enter_context(tc.psum_pool(name="ps", bufs=1))

        def tiles(name, count, shape, dtype):
            names = ["%s%d" % (name, i) for i in range(count)]
            return [sb.tile(shape, dtype, name=each, tag=each, align_bytes=64) for each in names]

        idx = sb.tile([P, S // 16], U16, name="idx")
        idx2 = sb.tile([P, S // 16], U16, name="idx2")
        tab_w = tiles("tab_w", 2, [P, T], U32)
        tab_s = sb.tile([P, T], U8, name="tab_s", align_bytes=64)
        v_w = tiles("v_w", 2, [P, S], U32)
        sel_s = sb.tile([P, S], U8, name="sel_s", align_bytes=64)
        v_s = tiles("v_s", 2, [P, S], U8)
        raw = tiles("raw", RAW_RING, [P, PACK, PASS], F32)
        w_bf = tiles("w_bf", 2, [P, PASS * PACK], BF16)
        w1_w = tiles("w1_w", 4, [P, PASS], U32)
        w1_s = tiles("w1_s", 4, [P, PASS], U8)
        w3_w = []
        w3_s = tiles("w3_s", 2, [P, N], U8)
        w2_w = sb.tile([P, 2, N], U32, name="w2_w", align_bytes=64)
        w2_s = sb.tile([P, 2, N], U8, name="w2_s", align_bytes=64)
        wgo_sb = sb.tile([P, S], F32, name="wgo_sb", align_bytes=64)
        gates = tiles("gates", GATE_RING, [P, T], F32)
        s_sel = tiles("s_sel", SEL_RING, [P, HALF], F32)
        part = tiles("part", PART_RING, [P, HALF], F32)
        d_rows = tiles("d_rows", 3, [P, PACK, HALF], BF16)
        d_bf = tiles("d_bf", 2, [P, HALF * PACK], BF16)
        d_w = {}
        d_s = tiles("d_s", 4, [P, HALF], U8)
        lim = tiles("lim", 2, [P, HALF], F32)
        y_sb = tiles("y_sb", 3, [P, HALF], F32)
        pages = tiles("page", 3, [P, T2], F32)
        h_ps = [ps.tile([P, HALF], F32, name="h_ps%d" % i) for i in range(H_BANKS)]
        ym_ps = [ps.tile([P, HALF], F32, name="ym_ps%d" % i) for i in range(2)]
        yr_ps = [ps.tile([P, HALF], F32, name="yr_ps%d" % i) for i in range(2)]

        def load_scale_rows(queue, plane, rows):
            nc.vector.memset(plane[:].rearrange("p a c -> p (a c)").bitcast(I32), 0)
            for q in range(4):
                queue.dma_start(
                    out=plane[32 * q : 32 * q + 4, :, :].bitcast(I32),
                    in_=rows[:, 4 * q : 4 * q + 4, :].rearrange("a r c -> r a c").bitcast(I32),
                )

        def load_weight(i):
            if i < 4:
                b, a = divmod(i, 2)
                rows = w1[a * PASS : (a + 1) * PASS, b * PASS : (b + 1) * PASS]
            else:
                rows = w3[(i - 4) * PASS : (i - 3) * PASS, :]
            nc.sync.dma_start(out=raw[i % RAW_RING][:], in_=rows.rearrange("(p j) c -> p j c", j=PACK))

        def cast_weight(i):
            src, grouped = raw[i % RAW_RING], w_bf[i % 2]
            if i < 4:
                nc.scalar.copy(
                    out=grouped[:].rearrange("p (t m j) -> p m j t", t=PACK, j=PACK),
                    in_=src[:].rearrange("p j (m t) -> p m j t", t=PACK),
                )
            else:
                nc.scalar.copy(
                    out=grouped[:].rearrange("p (c i j) -> p c j i", i=PACK, j=PACK),
                    in_=src[:].rearrange("p j (c i) -> p c j i", i=PACK),
                )

        def quantize_weight(i):
            words, scales = (w1_w[i][:], w1_s[i]) if i < 4 else (w3_w[i - 4], w3_s[i - 4])
            nc.vector.quantize_mx(out=words.bitcast(E4M3), scales=scales[:], in_=w_bf[i % 2][:])

        def load_table(a):
            nc.sync.dma_start(
                out=tab_w[a][:].bitcast(I32), in_=tab_words[a].rearrange("p c i -> p (c i)").bitcast(I32)
            )

        def load_gates(g):
            b, t = divmod(g, PACK)
            rows = sT[b * PASS : (b + 1) * PASS, :].rearrange("(p t) c -> p t c", t=PACK)
            nc.sync.dma_start(out=gates[g % GATE_RING][:], in_=rows[:, t, :])

        steps = [(g, half) for g in range(6) for half in range(2)] + [(6, 0), (7, 0), (6, 1), (7, 1)]

        def sel_slot(u):
            return s_sel[min(u, LATE) % SEL_RING]

        def gather_gates(u):
            g, half = steps[u]
            offsets = idx[:, half * HALF // 16 : (half + 1) * HALF // 16]
            nc.vector.tensor_copy(out=sel_slot(u)[:], in_=gates[g % GATE_RING][:].indirect(offsets))

        def gate_step(u):
            g, half = steps[u]
            b, t = divmod(g, PACK)
            cols = slice(half * HALF, (half + 1) * HALF)
            bank = h_ps[u % H_BANKS]
            for a in range(2):
                nc.tensor.matmul_mx(
                    out=bank[:],
                    lhsT=w1_w[2 * b + a][:, t * P : (t + 1) * P].bitcast(E4M3),
                    lhsT_scale=w1_s[2 * b + a][:, t * P : (t + 1) * P],
                    rhs=v_w[a][:, cols].bitcast(E5M2),
                    rhs_scale=v_s[a][:, cols],
                    start=(a == 0),
                    stop=(a == 1),
                )
            nc.vector.scalar_tensor_tensor(
                out=part[u % PART_RING][:], in0=sel_slot(u)[:], scalar=1.0, in1=bank[:],
                op0=ALU.subtract, op1=ALU.mult,
            )
            (nc.gpsimd if u < LATE else nc.vector).tensor_tensor(
                out=d_rows[(2 * b + half) % 3][:, t, :], in0=part[u % PART_RING][:], in1=sel_slot(u)[:], op=ALU.mult
            )

        def interleave_d(b, half):
            nc.scalar.activation(
                out=d_bf[(2 * b + half) % 3][:].rearrange("p (c t) -> p c t", t=PACK),
                in_=d_rows[(2 * b + half) % 3][:].rearrange("p t c -> p c t"),
                func=ACT.Copy,
                scale=-1.0,
            )

        def quantize_d(b, half):
            nc.vector.quantize_mx(
                out=d_w[b, half].bitcast(E4M3), scales=d_s[2 * b + half][:], in_=d_bf[(2 * b + half) % 3][:]
            )

        def product(bank, words, scales, nt, half):
            rows = slice(nt * P, (nt + 1) * P)
            for b in range(2):
                nc.tensor.matmul_mx(
                    out=bank[:],
                    lhsT=words[b][:, rows].bitcast(E4M3),
                    lhsT_scale=scales[b][:, rows],
                    rhs=d_w[b, half].bitcast(E4M3),
                    rhs_scale=d_s[2 * b + half][:],
                    start=(b == 0),
                    stop=(b == 1),
                )

        nc.sync.dma_start(idx[:], offs)
        for q in range(4):
            nc.scalar.dma_start(
                out=tab_s[32 * q + 24 : 32 * q + 32, :].bitcast(I32),
                in_=tab_scales[:, 4 * q : 4 * q + 4, :].bitcast(I32),
            )
            nc.vector.memset(tab_s[32 * q : 32 * q + 24, :].bitcast(I32), 0)
        load_weight(0)
        load_table(0)
        load_weight(1)
        load_table(1)
        load_gates(0)
        load_gates(1)
        nc.vector.tensor_copy(out=sel_s[:], in_=tab_s[:].indirect(idx[:]))
        for a in range(2):
            first = 24 + 4 * a
            nc.vector.memset(v_s[a][:].bitcast(I32), 0)
            nc.scalar.dma_start(out=v_s[a][0 : P - first, :].bitcast(I32), in_=sel_s[first:P, :].bitcast(I32))
        for page in pages:
            nc.vector.memset(page[:], 0.0)
        for a in range(2):
            nc.vector.tensor_copy(out=v_w[a][:], in_=tab_w[a][:].indirect(idx[:]))
            cast_weight(a)
            quantize_weight(a)
        pages.append(sb.tile([P, T2], F32, name="page3", tag="tab_w0", align_bytes=64))
        nc.gpsimd.memset(pages[3][:], 0.0)
        d_bf.append(sb.tile([P, HALF * PACK], BF16, name="d_bf2", tag="tab_w1", align_bytes=64))
        load_weight(2)
        load_weight(3)
        for g in (2, 3, 4, 5):
            load_gates(g)
        load_weight(4)
        load_gates(6)
        load_weight(5)
        load_gates(7)
        load_scale_rows(nc.sync, w2_s, w2_scales)
        nc.sync.dma_start(out=w2_w[:].bitcast(I32), in_=w2_words.rearrange("a p c i -> p a (c i)").bitcast(I32))
        nc.sync.dma_start(out=wgo_sb[:], in_=wgo)
        nc.sync.dma_start(idx2[:], offs2)

        gather_gates(0)
        for u in range(LATE + 1):
            if u < LATE:
                gather_gates(u + 1)
            gate_step(u)
            if u in (3, 4):
                cast_weight(u - 1)
                quantize_weight(u - 1)
            if u in (6, 7):
                interleave_d(0, u - 6)
            if u in (10, 11):
                cast_weight(u - 6)
        interleave_d(1, 0)

        gather_gates(LATE + 1)
        late_w = sb.tile([P, 3, HALF], U32, name="late_w", tag="gates6", align_bytes=64)
        w3_w.extend([late_w[:, 0, :], late_w[:, 1, :]])
        d_rest = tiles("d_w", 2, [P, HALF], U32)
        d_w[0, 0], d_w[1, 0], d_w[1, 1] = late_w[:, 2, :], d_rest[0][:], d_rest[1][:]
        quantize_d(0, 0)
        quantize_weight(4)
        quantize_weight(5)
        quantize_d(1, 0)
        gate_step(LATE + 1)
        gather_gates(LATE + 2)
        last_w = sb.tile([P, HALF], U32, name="last_w", tag="gates7", align_bytes=64)
        d_w[0, 1] = last_w[:]
        quantize_d(0, 1)
        gate_step(LATE + 2)
        interleave_d(1, 1)

        w2_parts = [w2_w[:, 0, :], w2_w[:, 1, :]], [w2_s[:, 0, :], w2_s[:, 1, :]]
        ym_sb = sb.tile([P, 2, HALF], F32, name="ym_sb", tag="raw2", align_bytes=64)
        factor = sb.tile([P, 2, HALF], F32, name="factor", tag="raw3", align_bytes=64)
        units = [(nt, half) for half in range(2) for nt in range(N // P)]
        for u, (nt, half) in enumerate(units):
            cols = slice(half * HALF, (half + 1) * HALF)
            product(yr_ps[u % 2], w3_w, w3_s, nt, half)
            nc.scalar.activation(out=lim[u % 2][:], in_=yr_ps[u % 2][:], func=ACT.Tanh)
            product(ym_ps[u % 2], *w2_parts, nt, half)
            (nc.vector if u == 0 else nc.gpsimd).tensor_tensor(
                out=factor[:, u % 2, :], in0=lim[u % 2][:], in1=wgo_sb[:, cols], op=ALU.mult
            )
            if u == 2:
                quantize_d(1, 1)
                y_held = sb.tile([P, 2, HALF], F32, name="y_held", tag="d_bf0", align_bytes=64)
            y = y_held[:, u - 2, :] if u in (2, 3) else y_sb[u % 3][:]
            if u in (0, 2):
                nc.vector.tensor_tensor(out=y, in0=ym_ps[0][:], in1=factor[:, 0, :], op=ALU.mult)
            else:
                nc.scalar.copy(out=ym_sb[:, u % 2, :], in_=ym_ps[u % 2][:])
                nc.gpsimd.tensor_tensor(out=y, in0=ym_sb[:, u % 2, :], in1=factor[:, u % 2, :], op=ALU.mult)
            nc.vector.tensor_copy(
                out=pages[nt][:].indirect(idx2[:, half * HALF // 16 : (half + 1) * HALF // 16]), in_=y
            )
            if half == 1:
                nc.sync.dma_start(out=out[nt * P : (nt + 1) * P, :], in_=pages[nt][:])
